import numpy as np
import ml_dtypes


def mxq(x, axis, fmt="e4m3"):
    dtype, down = {"e4m3": (ml_dtypes.float8_e4m3fn, 7), "e5m2": (ml_dtypes.float8_e5m2, 14)}[fmt]
    v = np.moveaxis(np.asarray(x, np.float32).astype(ml_dtypes.bfloat16).astype(np.float64), axis, -1)
    blocks = v.reshape(v.shape[:-1] + (-1, 32))
    amax = np.abs(blocks).max(-1, keepdims=True)
    byte = np.maximum(np.where(amax > 0, np.frexp(amax)[1] - 1 + 127, 0) - down, 1)
    scale = np.exp2(byte - 127.0)
    codes = (blocks / scale).astype(np.float32).astype(dtype).astype(np.float64)
    return np.moveaxis((codes * scale).reshape(v.shape), -1, axis)


WIDE = False


def mx_kscale(k):
    if not WIDE:
        return np.ones(k)
    levels = np.array([10, -10, 5, -5, 0])
    if k % 512:
        return np.exp2(np.random.permutation(np.resize(levels, k // 32))).repeat(32)
    a = np.empty((k // 512, 16))
    for p in range(k // 512):
        a[p, :8] = np.random.permutation(np.resize(levels, 8))
        for g in range(8):
            far = levels[np.abs(levels - a[p, g]) >= 10]
            a[p, g + 8] = far[np.random.randint(len(far))]
    return np.exp2(a.ravel()).repeat(32)


BF16 = ml_dtypes.bfloat16


def bf(x):
    return np.asarray(x, np.float32).astype(BF16)


def f64(x):
    return np.asarray(x).astype(np.float64)


E2M1 = np.array([0.0, 0.5, 1.0, 1.5, 2.0, 3.0, 4.0, 6.0, -0.0, -0.5, -1.0, -1.5, -2.0, -3.0, -4.0, -6.0])


def pack_weight(w, fmt):
    k, n = w.shape
    w = f64(bf(w)).reshape(k // 32, 32, n)
    amax = np.abs(w).max(1)
    if fmt == "e4m3":
        byte = np.frexp(amax)[1] - 1 + 127 - 7
    else:
        mant, ex = np.frexp(amax / 6.0)
        byte = np.where(mant > 0.5, ex, ex - 1) + 127
    byte = np.clip(np.where(amax > 0, byte, 1), 1, 254)
    scaled = (w * np.exp2(127.0 - byte)[:, None, :]).reshape(k, n).astype(np.float32)
    by_word = np.ascontiguousarray(scaled.reshape(k // 512, 128, 4, n).transpose(0, 1, 3, 2))
    if fmt == "e4m3":
        words = by_word.astype(ml_dtypes.float8_e4m3fn).view(np.uint8)
    else:
        c = by_word.astype(ml_dtypes.float4_e2m1fn).view(np.uint8) & 0xF
        words = c[..., 0::2] | (c[..., 1::2] << 4)
    return np.ascontiguousarray(words), np.ascontiguousarray(byte.astype(np.uint8).reshape(k // 512, 16, n))


def unpack_weight(words, scales, fmt):
    g, p, n, _ = words.shape
    if fmt == "e4m3":
        vals = np.ascontiguousarray(words).view(ml_dtypes.float8_e4m3fn).astype(np.float64)
    else:
        nib = np.empty((g, p, n, 4), np.uint8)
        nib[..., 0::2] = words & 0xF
        nib[..., 1::2] = words >> 4
        vals = E2M1[nib]
    vals = vals * np.repeat(np.exp2(scales.astype(np.float64) - 127.0), 8, axis=1)[..., None]
    return vals.transpose(0, 1, 3, 2).reshape(g * 512, n)
def pack4(w):
    words, scales = pack_weight(w, "e2m1")
    return words.reshape(words.shape[0], 128, -1), scales


def unpack4(words, scales):
    return unpack_weight(words.reshape(words.shape[0], 128, -1, 2), scales, "e2m1")


S, D, M, J = 1024, 1024, 1024, 1024


def softplus(v):
    return np.maximum(v, 0.0) + np.log(1.0 + np.exp(-np.abs(v)))


def draw0():
    s, t = mx_kscale(D), mx_kscale(M)
    x = np.random.standard_normal((S, D))
    wl = np.random.standard_normal((D, M)) / np.sqrt(D)
    wu = np.random.standard_normal((D, M)) / np.sqrt(D)
    delta = np.random.standard_normal((S, M))
    prev = np.random.standard_normal((S, M))
    g = 1.0 + 0.1 * np.random.standard_normal(M)
    r = np.random.standard_normal((M, J)) / np.sqrt(M)
    wl_words, wl_scales = pack4(wl / s[:, None])
    wu_words, wu_scales = pack4(wu / s[:, None])
    return {"x": bf(x * s), "wl_words": wl_words, "wl_scales": wl_scales, "wu_words": wu_words, "wu_scales": wu_scales, "delta": bf(delta),
            "prev": bf(prev), "g": bf(g * t), "r": bf(r / t[:, None])}


def core(x, wl_words, wl_scales, wu_words, wu_scales, delta, prev, g, r):
    xq = mxq(f64(x), 1, "e4m3")
    lo = f64(delta) - softplus(xq @ unpack4(wl_words, wl_scales))
    up = f64(delta) + softplus(xq @ unpack4(wu_words, wu_scales))
    hold = np.minimum(np.maximum(f64(prev), lo), up)
    pos = hold * f64(g)[None, :]
    return mxq(pos, 1, "e4m3") @ mxq(f64(r), 0, "e4m3")


def e4m3fn_bytes(y):
    return np.clip(np.asarray(y, np.float64), -448.0, 448.0).astype(np.float32).astype(ml_dtypes.float8_e4m3fn).view(np.uint8)


def e4m3fn_values(b):
    return np.asarray(b, np.uint8).view(ml_dtypes.float8_e4m3fn).astype(np.float64)


def setup_inputs():
    d = draw0()
    x0 = np.asarray(d['x']).astype(np.float64)
    s = (np.max(np.abs(x0), axis=(0,), keepdims=True) / 448.0).astype(np.float32)
    out = {}
    for k, v in d.items():
        if k == 'x':
            out['x_bytes'] = e4m3fn_bytes(x0 / s.astype(np.float64))
            out['x_scale'] = s
        else:
            out[k] = v
    return out


def reference(x_bytes, x_scale, wl_words, wl_scales, wu_words, wu_scales, delta, prev, g, r):
    return core(e4m3fn_values(x_bytes) * x_scale.astype(np.float64), wl_words, wl_scales, wu_words, wu_scales, delta, prev, g, r)

@@ -1,0 +1,297 @@
+from contextlib import ExitStack
+
+import concourse.mybir as mybir
+from concourse.masks import make_identity
+
+F32 = mybir.dt.float32
+BF16 = mybir.dt.bfloat16
+I32 = mybir.dt.int32
+U32 = mybir.dt.uint32
+U8 = mybir.dt.uint8
+FP8 = mybir.dt.float8_e4m3fn
+FP8X4 = mybir.dt.float8_e4m3fn_x4
+FP4X4 = mybir.dt.float4_e2m1fn_x4
+ACT = mybir.ActivationFunctionType
+ALU = mybir.AluOpType
+
+P = 128
+DIM = 1024
+TILES = DIM // P
+KP = 512
+PASSES = DIM // KP
+LN_FLOOR = 2.0 ** -60
+FLOPS = 3 * 2 * DIM * DIM * DIM
+
+
+def tile_notransactionbandhedgepnl_w4_kernel(tc, x_bytes, x_scale, wl_words, wl_scales, wu_words, wu_scales, delta, prev, g, r, out):
+    nc = tc.nc
+    with ExitStack() as ctx:
+        keep = ctx.enter_context(tc.tile_pool(name="keep", bufs=1))
+        work = ctx.enter_context(tc.tile_pool(name="work", bufs=2))
+        psum = ctx.enter_context(tc.psum_pool(name="psum", bufs=2))
+        ctx.enter_context(tc.manual_schedule())
+
+        ident32 = keep.tile([P, P], F32)
+        make_identity(nc, ident32[:])
+        ident16 = keep.tile([P, P], BF16)
+        make_identity(nc, ident16[:])
+        ln_floor = keep.tile([P, 1], F32)
+        nc.gpsimd.memset(ln_floor[:], LN_FLOOR)
+
+        w_words, w_planes = [], []
+        for w in range(2):
+            w_words.append(keep.tile([P, PASSES, 2 * DIM], U8, name="w_words%d" % w, align_bytes=64))
+            w_planes.append(keep.tile([P, PASSES, DIM], U8, name="w_plane%d" % w, align_bytes=64))
+            nc.vector.memset(w_planes[w][:].bitcast(I32), 0)
+
+        def load_rows(src, first, count, dtype, tag, bufs):
+            dst = work.tile([P, count, DIM], dtype, name=tag, tag=tag, bufs=bufs)
+            nc.sync.dma_start(out=dst[:], in_=src[first * P:(first + count) * P, :].rearrange("(n p) k -> p n k", p=P))
+            return [dst[:, n, :] for n in range(count)]
+
+        def load_weight(w, words, scales):
+            nc.sync.dma_start(out=w_words[w][:].bitcast(I32), in_=words.rearrange("g p n -> p g n").bitcast(I32))
+            for q in range(4):
+                nc.sync.dma_start(
+                    out=w_planes[w][32 * q:32 * q + 4, :, :].bitcast(I32),
+                    in_=scales[:, 4 * q:4 * q + 4, :].rearrange("g r n -> r g n").bitcast(I32),
+                )
+
+        x_rows = load_rows(x_bytes, 0, 1, U8, "xb_a", 1)
+        x_scale_all = keep.tile([P, DIM], F32)
+        nc.sync.dma_start(out=x_scale_all[:], in_=x_scale.rearrange("o k -> (o k)").partition_broadcast(P))
+        load_weight(0, wl_words, wl_scales)
+        x_rows = x_rows + load_rows(x_bytes, 1, 3, U8, "xb_b", 1)
+        load_weight(1, wu_words, wu_scales)
+        x_rows = x_rows + load_rows(x_bytes, 4, 4, U8, "xb_c", 1)
+        delta_rows, prev_rows = [], []
+        for pair in range(2):
+            delta_rows.extend(load_rows(delta, 2 * pair, 2, BF16, "delta_rows", 4))
+            prev_rows.extend(load_rows(prev, 2 * pair, 2, BF16, "prev_rows", 2))
+        r_raw = []
+        for h in range(PASSES):
+            raw = keep.tile([P, 4, DIM], BF16, name="r_raw%d" % h)
+            nc.sync.dma_start(out=raw[:], in_=r[h * KP:(h + 1) * KP, :].rearrange("(p t) j -> p t j", t=4))
+            r_raw.append(raw)
+        g_cols = keep.tile([P, PASSES, 4], BF16)
+        nc.sync.dma_start(out=g_cols[:], in_=g.rearrange("(h p t) -> p h t", p=P, t=4))
+        for pair in range(2, 4):
+            delta_rows.extend(load_rows(delta, 2 * pair, 2, BF16, "delta_rows", 4))
+
+        x_wide, x_turned, x_grouped, x_codes, x_planes = {}, {}, {}, {}, {}
+        logsig, gap, lower, upper, moved, held, pos, pos_codes, pos_planes, ab, result = {}, {}, {}, {}, {}, {}, {}, {}, {}, {}, {}
+        r_grouped = {}
+        r_codes = keep.tile([P, PASSES, DIM], U32, align_bytes=64)
+        r_planes = keep.tile([P, PASSES, DIM], U8, align_bytes=64)
+
+        def x_multiply(i):
+            x_wide[i] = work.tile([P, DIM], BF16, name="x_wide", bufs=3)
+            nc.vector.tensor_tensor(out=x_wide[i][:], in0=x_rows[i].bitcast(FP8), in1=x_scale_all[:], op=ALU.mult)
+
+        def x_turn(i):
+            x_turned[i] = psum.tile([P, PASSES, 2, P], F32, name="x_turned", tag="xo")
+            words = x_wide[i][:].bitcast(F32)
+            for h in range(PASSES):
+                for u in range(2):
+                    nc.tensor.transpose(x_turned[i][:, h, u, :], words[:, 256 * h + u:256 * (h + 1):2], ident32[:])
+
+        def x_group(i):
+            x_grouped[i] = work.tile([P, DIM], BF16, name="x_grouped", align_bytes=64)
+            nc.scalar.copy(
+                out=x_grouped[i][:].bitcast(F32).rearrange("p (h s u) -> p h s u", h=PASSES, u=2),
+                in_=x_turned[i][:].rearrange("p h u s -> p h s u"),
+            )
+
+        def x_quantize(i):
+            x_codes[i] = work.tile([P, PASSES * P], U32, name="x_codes", bufs=TILES, align_bytes=64)
+            x_planes[i] = work.tile([P, PASSES * P], U8, name="x_planes", bufs=TILES, align_bytes=64)
+            nc.vector.quantize_mx(out=x_codes[i][:].bitcast(FP8X4), scales=x_planes[i][:], in_=x_grouped[i][:])
+
+        def project(i, h, w):
+            ab[i, h, w] = psum.tile([P, KP], F32, name="ab", bufs=4)
+            for k in range(PASSES):
+                nc.tensor.matmul_mx(
+                    out=ab[i, h, w][:],
+                    lhsT=x_codes[i][:, k * P:(k + 1) * P].bitcast(FP8X4),
+                    lhsT_scale=x_planes[i][:, k * P:(k + 1) * P],
+                    rhs=w_words[w][:, k, 2 * h * KP:2 * (h + 1) * KP].bitcast(FP4X4),
+                    rhs_scale=w_planes[w][:, k, h * KP:(h + 1) * KP],
+                    start=(k == 0),
+                    stop=(k == PASSES - 1),
+                )
+
+        def by_slot(ap):
+            return ap.rearrange("s (p t) -> s t p", t=4)
+
+        def slots(ap):
+            return ap.rearrange("s (t p) -> s t p", t=4)
+
+        def sigmoid(i, h, w):
+            if (h, w) == (0, 0):
+                logsig[i] = work.tile([P, PASSES, 2, KP], F32, name="logsig", bufs=TILES)
+            nc.scalar.activation(out=slots(logsig[i][:, h, w, :]), in_=by_slot(ab[i, h, w][:]), func=ACT.Sigmoid, scale=-1.0)
+
+        def log(i, h):
+            nc.scalar.activation(out=logsig[i][:, h, :, :], in_=logsig[i][:, h, :, :], func=ACT.Ln, bias=ln_floor[:])
+
+        def subtract(i):
+            gap[i] = work.tile([P, DIM], F32, name="gap", bufs=TILES)
+            nc.vector.tensor_tensor(
+                out=gap[i][:].rearrange("s (h t p) -> s h t p", h=PASSES, t=4),
+                in0=prev_rows[i].rearrange("s (h p t) -> s h t p", h=PASSES, t=4),
+                in1=delta_rows[i].rearrange("s (h p t) -> s h t p", h=PASSES, t=4),
+                op=ALU.subtract,
+            )
+
+        def r_group(h, c):
+            r_grouped[h, c] = work.tile([P, KP, 4], BF16, name="r_grouped", align_bytes=64)
+            nc.vector.tensor_copy(
+                out=r_grouped[h, c][:].rearrange("p (c i) t -> p c t i", i=4),
+                in_=r_raw[h][:, :, c * KP:(c + 1) * KP].rearrange("p t (c i) -> p c t i", i=4),
+            )
+
+        def r_quantize(h, c):
+            cols = slice(c * KP, (c + 1) * KP)
+            nc.vector.quantize_mx(
+                out=r_codes[:, h, cols].bitcast(FP8X4),
+                scales=r_planes[:, h, cols],
+                in_=r_grouped[h, c][:].rearrange("p j t -> p (j t)"),
+            )
+
+        def lower_edge(i, h):
+            lower[i, h] = work.tile([P, KP], F32, name="lower")
+            nc.vector.scalar_tensor_tensor(
+                out=slots(lower[i, h][:]), in0=by_slot(ab[i, h, 0][:]), scalar=-1.0,
+                in1=slots(logsig[i][:, h, 0, :]), op0=ALU.mult, op1=ALU.min,
+            )
+
+        def upper_edge(i, h):
+            upper[i, h] = work.tile([P, KP], F32, name="upper")
+            nc.vector.scalar_tensor_tensor(
+                out=slots(upper[i, h][:]), in0=slots(logsig[i][:, h, 1, :]), scalar=-1.0,
+                in1=by_slot(ab[i, h, 1][:]), op0=ALU.mult, op1=ALU.max,
+            )
+
+        def clamp_below(i, h):
+            nc.vector.tensor_tensor(out=lower[i, h][:], in0=lower[i, h][:], in1=gap[i][:, h * KP:(h + 1) * KP], op=ALU.max)
+
+        def clamp_above(i, h):
+            moved[i, h] = work.tile([P, KP], F32, name="moved", bufs=3)
+            nc.vector.tensor_tensor(out=moved[i, h][:], in0=lower[i, h][:], in1=upper[i, h][:], op=ALU.min)
+
+        def turn_and_add(i, h):
+            held[i, h] = psum.tile([P, 4, P], F32, name="held")
+            for t in range(4):
+                nc.tensor.matmul(
+                    held[i, h][:, t, :], lhsT=delta_rows[i][:, h * KP + t:(h + 1) * KP:4], rhs=ident16[:],
+                    start=(t == 0), stop=False,
+                )
+            for t in range(4):
+                nc.tensor.matmul(
+                    held[i, h][:, t, :], lhsT=moved[i, h][:, t * P:(t + 1) * P], rhs=ident32[:],
+                    start=False, stop=(t == 3), is_transpose=True,
+                )
+
+        def scale_by_g(i, h):
+            if h == 0:
+                pos[i] = work.tile([P, PASSES, P, 4], BF16, name="pos", align_bytes=64)
+            nc.vector.tensor_tensor(
+                out=pos[i][:, h, :, :], in0=held[i, h][:].rearrange("p t s -> p s t"),
+                in1=g_cols[:, h, :].unsqueeze(1).to_broadcast([P, P, 4]), op=ALU.mult,
+            )
+
+        def pos_quantize(i):
+            pos_codes[i] = work.tile([P, PASSES * P], U32, name="pos_codes", bufs=3, align_bytes=64)
+            pos_planes[i] = work.tile([P, PASSES * P], U8, name="pos_planes", bufs=3, align_bytes=64)
+            nc.vector.quantize_mx(
+                out=pos_codes[i][:].bitcast(FP8X4), scales=pos_planes[i][:],
+                in_=pos[i][:].rearrange("p h s t -> p (h s t)"),
+            )
+
+        def settle(i):
+            result[i] = work.tile([P, DIM], F32, name="result")
+            for c in range(2):
+                cols = slice(c * KP, (c + 1) * KP)
+                acc = psum.tile([P, KP], F32, name="acc", tag="xo")
+                for h in range(PASSES):
+                    nc.tensor.matmul_mx(
+                        out=acc[:],
+                        lhsT=pos_codes[i][:, h * P:(h + 1) * P].bitcast(FP8X4),
+                        lhsT_scale=pos_planes[i][:, h * P:(h + 1) * P],
+                        rhs=r_codes[:, h, cols].bitcast(FP8X4),
+                        rhs_scale=r_planes[:, h, cols],
+                        start=(h == 0),
+                        stop=(h == PASSES - 1),
+                    )
+                nc.scalar.copy(out=result[i][:, cols], in_=acc[:])
+            nc.sync.dma_start(out=out[i * P:(i + 1) * P, :], in_=result[i][:])
+
+        r_pieces = [(h, c) for c in range(2) for h in range(PASSES)]
+        x_multiply(0)
+        x_turn(0)
+        x_group(0)
+        x_multiply(1)
+        x_turn(1)
+        x_group(1)
+        x_quantize(0)
+        x_multiply(2)
+        x_quantize(1)
+        for i in range(TILES):
+            if i + 2 < TILES:
+                x_turn(i + 2)
+            for h in range(PASSES):
+                for w in range(2):
+                    project(i, h, w)
+                    sigmoid(i, h, w)
+            if i + 2 < TILES:
+                x_group(i + 2)
+            if i + 3 < TILES:
+                x_multiply(i + 3)
+            subtract(i)
+            if i in (1, 3):
+                prev_rows.extend(load_rows(prev, i + 3, 2, BF16, "prev_rows", 2))
+            if i + 2 < TILES:
+                x_quantize(i + 2)
+            if i >= 5:
+                r_quantize(*r_pieces[i - 5])
+            if i >= 4:
+                r_group(*r_pieces[i - 4])
+        log(0, 0)
+        log(0, 1)
+        for w in range(2):
+            project(0, 0, w)
+        r_quantize(*r_pieces[3])
+
+        for i in range(TILES + 2):
+            now, last = i < TILES, 1 <= i <= TILES
+            if i + 1 < TILES:
+                log(i + 1, 0)
+                log(i + 1, 1)
+            if last:
+                turn_and_add(i - 1, 1)
+            if now:
+                lower_edge(i, 0)
+            if last:
+                scale_by_g(i - 1, 0)
+            if now:
+                upper_edge(i, 0)
+                for w in range(2):
+                    project(i, 1, w)
+            if last:
+                scale_by_g(i - 1, 1)
+            if i + 1 < TILES:
+                for w in range(2):
+                    project(i + 1, 0, w)
+            if i >= 2:
+                settle(i - 2)
+            if now:
+                clamp_below(i, 0)
+                lower_edge(i, 1)
+                clamp_above(i, 0)
+                turn_and_add(i, 0)
+                upper_edge(i, 1)
+                clamp_below(i, 1)
+            if last:
+                pos_quantize(i - 1)
+            if now:
+                clamp_above(i, 1)

@@ -32,37 +32,42 @@ def tile_notransactionbandhedgepnl_w4_kernel(tc, x_bytes, x_scale, wl_words, wl_
         ctx.enter_context(tc.manual_schedule())
 
         ident32 = keep.tile([P, P], F32)
-        make_identity(nc, ident32[:])
-        ident16 = keep.tile([P, P], BF16)
-        make_identity(nc, ident16[:])
-        ln_floor = keep.tile([P, 1], F32)
-        nc.gpsimd.memset(ln_floor[:], LN_FLOOR)
-
+        nc.vector.memset(ident32[:], 0.0)
         w_words, w_planes = [], []
         for w in range(2):
             w_words.append(keep.tile([P, PASSES, 2 * DIM], U8, name="w_words%d" % w, align_bytes=64))
             w_planes.append(keep.tile([P, PASSES, DIM], U8, name="w_plane%d" % w, align_bytes=64))
             nc.vector.memset(w_planes[w][:].bitcast(I32), 0)
+        ident16 = keep.tile([P, P], BF16)
+        nc.vector.memset(ident16[:], 0.0)
+        ln_floor = keep.tile([P, 1], F32)
+        nc.vector.memset(ln_floor[:], LN_FLOOR)
+        make_identity(nc, ident32[:], nomemset=True)
+        make_identity(nc, ident16[:], nomemset=True)
 
         def load_rows(src, first, count, dtype, tag, bufs):
             dst = work.tile([P, count, DIM], dtype, name=tag, tag=tag, bufs=bufs)
             nc.sync.dma_start(out=dst[:], in_=src[first * P:(first + count) * P, :].rearrange("(n p) k -> p n k", p=P))
             return [dst[:, n, :] for n in range(count)]
 
-        def load_weight(w, words, scales):
+        def load_words(w, words):
             nc.sync.dma_start(out=w_words[w][:].bitcast(I32), in_=words.rearrange("g p n -> p g n").bitcast(I32))
+
+        def load_plane(w, scales):
             for q in range(4):
                 nc.sync.dma_start(
                     out=w_planes[w][32 * q:32 * q + 4, :, :].bitcast(I32),
                     in_=scales[:, 4 * q:4 * q + 4, :].rearrange("g r n -> r g n").bitcast(I32),
                 )
 
+        scale_cols = keep.tile([P, PASSES, 4], F32)
+        nc.sync.dma_start(out=scale_cols[:], in_=x_scale.rearrange("o (h p t) -> p (o h) t", p=P, t=4))
         x_rows = load_rows(x_bytes, 0, 1, U8, "xb_a", 1)
-        x_scale_all = keep.tile([P, DIM], F32)
-        nc.sync.dma_start(out=x_scale_all[:], in_=x_scale.rearrange("o k -> (o k)").partition_broadcast(P))
-        load_weight(0, wl_words, wl_scales)
+        load_words(0, wl_words)
+        load_plane(0, wl_scales)
         x_rows = x_rows + load_rows(x_bytes, 1, 3, U8, "xb_b", 1)
-        load_weight(1, wu_words, wu_scales)
+        load_words(1, wu_words)
+        load_plane(1, wu_scales)
         x_rows = x_rows + load_rows(x_bytes, 4, 4, U8, "xb_c", 1)
         delta_rows, prev_rows = [], []
         for pair in range(2):
@@ -79,25 +84,39 @@ def tile_notransactionbandhedgepnl_w4_kernel(tc, x_bytes, x_scale, wl_words, wl_
             delta_rows.extend(load_rows(delta, 2 * pair, 2, BF16, "delta_rows", 4))
 
         x_wide, x_turned, x_grouped, x_codes, x_planes = {}, {}, {}, {}, {}
-        logsig, gap, lower, upper, moved, held, pos, pos_codes, pos_planes, ab, result = {}, {}, {}, {}, {}, {}, {}, {}, {}, {}, {}
+        logsig, gap, lower, upper, moved, held, pos, pos_codes, pos_planes, ab, sums = {}, {}, {}, {}, {}, {}, {}, {}, {}, {}, {}
         r_grouped = {}
+        g_wide = keep.tile([P, PASSES, 4], F32)
         r_codes = keep.tile([P, PASSES, DIM], U32, align_bytes=64)
         r_planes = keep.tile([P, PASSES, DIM], U8, align_bytes=64)
 
+        scale_rows = keep.tile([P, PASSES, 2, P, 2], F32)
+
+        def spread_scale(h):
+            spread = psum.tile([P, 4, P], F32, name="spread", tag="ab", bufs=4)
+            for t in range(4):
+                nc.tensor.transpose(spread[:, t, :], scale_cols[:, h, t:t + 1].to_broadcast([P, P]), ident32[:])
+            nc.scalar.copy(out=scale_rows[:, h, :, :, :], in_=spread[:].rearrange("s (u e) p -> s u p e", e=2))
+
         def x_multiply(i):
-            x_wide[i] = work.tile([P, DIM], BF16, name="x_wide", bufs=3)
-            nc.vector.tensor_tensor(out=x_wide[i][:], in0=x_rows[i].bitcast(FP8), in1=x_scale_all[:], op=ALU.mult)
+            x_wide[i] = work.tile([P, PASSES, 2, P, 2], BF16, name="x_wide", bufs=4)
+            for h in range(PASSES):
+                nc.vector.tensor_tensor(
+                    out=x_wide[i][:, h, :, :, :],
+                    in0=x_rows[i][:, h * KP:(h + 1) * KP].bitcast(FP8).rearrange("s (p u e) -> s u p e", u=2, e=2),
+                    in1=scale_rows[:, h, :, :, :], op=ALU.mult,
+                )
 
         def x_turn(i):
             x_turned[i] = psum.tile([P, PASSES, 2, P], F32, name="x_turned", tag="xo")
-            words = x_wide[i][:].bitcast(F32)
+            words = x_wide[i][:].rearrange("s h u p e -> s h u (p e)").bitcast(F32)
             for h in range(PASSES):
                 for u in range(2):
-                    nc.tensor.transpose(x_turned[i][:, h, u, :], words[:, 256 * h + u:256 * (h + 1):2], ident32[:])
+                    nc.tensor.transpose(x_turned[i][:, h, u, :], words[:, h, u, :], ident32[:])
 
-        def x_group(i):
+        def x_group(i, copy):
             x_grouped[i] = work.tile([P, DIM], BF16, name="x_grouped", align_bytes=64)
-            nc.scalar.copy(
+            copy(
                 out=x_grouped[i][:].bitcast(F32).rearrange("p (h s u) -> p h s u", h=PASSES, u=2),
                 in_=x_turned[i][:].rearrange("p h u s -> p h s u"),
             )
@@ -179,119 +198,163 @@ def tile_notransactionbandhedgepnl_w4_kernel(tc, x_bytes, x_scale, wl_words, wl_
             moved[i, h] = work.tile([P, KP], F32, name="moved", bufs=3)
             nc.vector.tensor_tensor(out=moved[i, h][:], in0=lower[i, h][:], in1=upper[i, h][:], op=ALU.min)
 
-        def turn_and_add(i, h):
+        def turn_delta(i, h):
             held[i, h] = psum.tile([P, 4, P], F32, name="held")
             for t in range(4):
                 nc.tensor.matmul(
                     held[i, h][:, t, :], lhsT=delta_rows[i][:, h * KP + t:(h + 1) * KP:4], rhs=ident16[:],
                     start=(t == 0), stop=False,
                 )
+
+        def turn_moved(i, h):
             for t in range(4):
                 nc.tensor.matmul(
                     held[i, h][:, t, :], lhsT=moved[i, h][:, t * P:(t + 1) * P], rhs=ident32[:],
                     start=False, stop=(t == 3), is_transpose=True,
                 )
 
-        def scale_by_g(i, h):
-            if h == 0:
+        def pos_tile(i):
+            if i not in pos:
                 pos[i] = work.tile([P, PASSES, P, 4], BF16, name="pos", align_bytes=64)
+            return pos[i]
+
+        def scale_by_g(i, h):
             nc.vector.tensor_tensor(
-                out=pos[i][:, h, :, :], in0=held[i, h][:].rearrange("p t s -> p s t"),
+                out=pos_tile(i)[:, h, :, :], in0=held[i, h][:].rearrange("p t s -> p s t"),
                 in1=g_cols[:, h, :].unsqueeze(1).to_broadcast([P, P, 4]), op=ALU.mult,
             )
 
-        def pos_quantize(i):
-            pos_codes[i] = work.tile([P, PASSES * P], U32, name="pos_codes", bufs=3, align_bytes=64)
-            pos_planes[i] = work.tile([P, PASSES * P], U8, name="pos_planes", bufs=3, align_bytes=64)
+        def scale_by_g_scalar(i, h):
+            apart = work.tile([P, 4, P], BF16, name="apart")
+            for t in range(4):
+                nc.scalar.activation(out=apart[:, t, :], in_=held[i, h][:, t, :], func=ACT.Copy, scale=g_wide[:, h, t:t + 1])
+            nc.scalar.copy(
+                out=pos_tile(i)[:, h, :, :].rearrange("p (c i) t -> p c t i", i=4),
+                in_=apart[:].rearrange("p t (c i) -> p c t i", i=4),
+            )
+
+        def pos_quantize(i, passes):
+            if i not in pos_codes:
+                pos_codes[i] = work.tile([P, PASSES * P], U32, name="pos_codes", bufs=3, align_bytes=64)
+                pos_planes[i] = work.tile([P, PASSES * P], U8, name="pos_planes", bufs=3, align_bytes=64)
+            cols = slice(passes.start * P, passes.stop * P)
             nc.vector.quantize_mx(
-                out=pos_codes[i][:].bitcast(FP8X4), scales=pos_planes[i][:],
-                in_=pos[i][:].rearrange("p h s t -> p (h s t)"),
+                out=pos_codes[i][:, cols].bitcast(FP8X4), scales=pos_planes[i][:, cols],
+                in_=pos[i][:, passes, :, :].rearrange("p h s t -> p (h s t)"),
+            )
+
+        def settle_pass(i, c, h):
+            cols = slice(c * KP, (c + 1) * KP)
+            if h == 0:
+                sums[i, c] = psum.tile([P, KP], F32, name="acc", **(dict(tag="ab", bufs=4) if i == TILES - 1 else dict(tag="xo")))
+            nc.tensor.matmul_mx(
+                out=sums[i, c][:],
+                lhsT=pos_codes[i][:, h * P:(h + 1) * P].bitcast(FP8X4),
+                lhsT_scale=pos_planes[i][:, h * P:(h + 1) * P],
+                rhs=r_codes[:, h, cols].bitcast(FP8X4),
+                rhs_scale=r_planes[:, h, cols],
+                start=(h == 0),
+                stop=(h == PASSES - 1),
             )
 
         def settle(i):
-            result[i] = work.tile([P, DIM], F32, name="result")
             for c in range(2):
-                cols = slice(c * KP, (c + 1) * KP)
-                acc = psum.tile([P, KP], F32, name="acc", tag="xo")
                 for h in range(PASSES):
-                    nc.tensor.matmul_mx(
-                        out=acc[:],
-                        lhsT=pos_codes[i][:, h * P:(h + 1) * P].bitcast(FP8X4),
-                        lhsT_scale=pos_planes[i][:, h * P:(h + 1) * P],
-                        rhs=r_codes[:, h, cols].bitcast(FP8X4),
-                        rhs_scale=r_planes[:, h, cols],
-                        start=(h == 0),
-                        stop=(h == PASSES - 1),
-                    )
-                nc.scalar.copy(out=result[i][:, cols], in_=acc[:])
-            nc.sync.dma_start(out=out[i * P:(i + 1) * P, :], in_=result[i][:])
+                    settle_pass(i, c, h)
 
-        r_pieces = [(h, c) for c in range(2) for h in range(PASSES)]
+        def store(i):
+            result = work.tile([P, DIM], F32, name="result")
+            for c in range(2):
+                nc.scalar.copy(out=result[:, c * KP:(c + 1) * KP], in_=sums[i, c][:])
+            nc.sync.dma_start(out=out[i * P:(i + 1) * P, :], in_=result[:])
+
+        def store_half(i, c, copy):
+            half = work.tile([P, KP], F32, name="half")
+            copy(out=half[:], in_=sums[i, c][:])
+            nc.sync.dma_start(out=out[i * P:(i + 1) * P, c * KP:(c + 1) * KP], in_=half[:])
+
+        for h in range(PASSES):
+            spread_scale(h)
         x_multiply(0)
         x_turn(0)
-        x_group(0)
+        x_group(0, nc.scalar.copy)
         x_multiply(1)
         x_turn(1)
-        x_group(1)
         x_quantize(0)
+        x_group(1, nc.vector.tensor_copy)
         x_multiply(2)
         x_quantize(1)
+        x_multiply(3)
+        r_pieces = [(h, c) for c in range(2) for h in range(PASSES)]
         for i in range(TILES):
-            if i + 2 < TILES:
-                x_turn(i + 2)
-            for h in range(PASSES):
-                for w in range(2):
+            for w in range(2):
+                for h in range(PASSES):
                     project(i, h, w)
                     sigmoid(i, h, w)
+                if w == 0 and i + 2 < TILES:
+                    x_turn(i + 2)
             if i + 2 < TILES:
-                x_group(i + 2)
-            if i + 3 < TILES:
-                x_multiply(i + 3)
-            subtract(i)
-            if i in (1, 3):
-                prev_rows.extend(load_rows(prev, i + 3, 2, BF16, "prev_rows", 2))
-            if i + 2 < TILES:
-                x_quantize(i + 2)
+                x_group(i + 2, nc.scalar.copy)
+            if i + 4 < TILES:
+                x_multiply(i + 4)
             if i >= 5:
                 r_quantize(*r_pieces[i - 5])
             if i >= 4:
                 r_group(*r_pieces[i - 4])
+            if i + 2 < TILES:
+                x_quantize(i + 2)
+            subtract(i)
+            if i in (1, 3):
+                prev_rows.extend(load_rows(prev, i + 3, 2, BF16, "prev_rows", 2))
+        nc.vector.tensor_copy(out=g_wide[:], in_=g_cols[:])
+        r_quantize(*r_pieces[3])
         log(0, 0)
         log(0, 1)
-        for w in range(2):
-            project(0, 0, w)
-        r_quantize(*r_pieces[3])
+        for h in range(PASSES):
+            for w in range(2):
+                project(0, h, w)
 
-        for i in range(TILES + 2):
-            now, last = i < TILES, 1 <= i <= TILES
-            if i + 1 < TILES:
+        last = TILES - 1
+        for i in range(TILES):
+            if i >= 1:
+                turn_moved(i - 1, 0)
+                turn_moved(i - 1, 1)
+                scale_by_g_scalar(i - 1, 1)
+            if i < last:
                 log(i + 1, 0)
                 log(i + 1, 1)
-            if last:
-                turn_and_add(i - 1, 1)
-            if now:
-                lower_edge(i, 0)
-            if last:
+            for h in range(PASSES):
+                lower_edge(i, h)
+                upper_edge(i, h)
+            if i < last:
+                for h in range(PASSES):
+                    for w in range(2):
+                        project(i + 1, h, w)
+            if i >= 1:
                 scale_by_g(i - 1, 0)
-            if now:
-                upper_edge(i, 0)
-                for w in range(2):
-                    project(i, 1, w)
-            if last:
-                scale_by_g(i - 1, 1)
-            if i + 1 < TILES:
-                for w in range(2):
-                    project(i + 1, 0, w)
             if i >= 2:
                 settle(i - 2)
-            if now:
-                clamp_below(i, 0)
-                lower_edge(i, 1)
-                clamp_above(i, 0)
-                turn_and_add(i, 0)
-                upper_edge(i, 1)
-                clamp_below(i, 1)
-            if last:
-                pos_quantize(i - 1)
-            if now:
-                clamp_above(i, 1)
+                store(i - 2)
+            turn_delta(i, 0)
+            turn_delta(i, 1)
+            clamp_below(i, 0)
+            if i == last:
+                pos_quantize(i - 1, slice(0, 2))
+                settle(i - 1)
+                store(i - 1)
+            clamp_below(i, 1)
+            clamp_above(i, 0)
+            if 1 <= i < last:
+                pos_quantize(i - 1, slice(0, 2))
+            if i == last:
+                turn_moved(i, 0)
+            clamp_above(i, 1)
+        turn_moved(last, 1)
+        for h in range(PASSES):
+            scale_by_g(last, h)
+        for h in range(PASSES):
+            pos_quantize(last, slice(h, h + 1))
+            for c in range(2):
+                settle_pass(last, c, h)
+        store_half(last, 0, nc.scalar.copy)
+        store_half(last, 1, nc.vector.tensor_copy)

@@ -20,6 +20,8 @@ TILES = DIM // P
 KP = 512
 PASSES = DIM // KP
 LN_FLOOR = 2.0 ** -60
+PARTS = (slice(0, 1), slice(1, 4))
+SCALAR_GROUPS = (0, 1)
 FLOPS = 3 * 2 * DIM * DIM * DIM
 
 
@@ -72,7 +74,7 @@ def tile_notransactionbandhedgepnl_w4_kernel(tc, x_bytes, x_scale, wl_words, wl_
         delta_rows, prev_rows = [], []
         for pair in range(2):
             delta_rows.extend(load_rows(delta, 2 * pair, 2, BF16, "delta_rows", 4))
-            prev_rows.extend(load_rows(prev, 2 * pair, 2, BF16, "prev_rows", 2))
+            prev_rows.extend(load_rows(prev, 2 * pair, 2, BF16, "prev_rows", 4))
         r_raw = []
         for h in range(PASSES):
             raw = keep.tile([P, 4, DIM], BF16, name="r_raw%d" % h)
@@ -82,6 +84,7 @@ def tile_notransactionbandhedgepnl_w4_kernel(tc, x_bytes, x_scale, wl_words, wl_
         nc.sync.dma_start(out=g_cols[:], in_=g.rearrange("(h p t) -> p h t", p=P, t=4))
         for pair in range(2, 4):
             delta_rows.extend(load_rows(delta, 2 * pair, 2, BF16, "delta_rows", 4))
+            prev_rows.extend(load_rows(prev, 2 * pair, 2, BF16, "prev_rows", 4))
 
         x_wide, x_turned, x_grouped, x_codes, x_planes = {}, {}, {}, {}, {}
         logsig, gap, lower, upper, moved, held, pos, pos_codes, pos_planes, ab, sums = {}, {}, {}, {}, {}, {}, {}, {}, {}, {}, {}
@@ -150,23 +153,26 @@ def tile_notransactionbandhedgepnl_w4_kernel(tc, x_bytes, x_scale, wl_words, wl_
                 logsig[i] = work.tile([P, PASSES, 2, KP], F32, name="logsig", bufs=TILES)
             nc.scalar.activation(out=slots(logsig[i][:, h, w, :]), in_=by_slot(ab[i, h, w][:]), func=ACT.Sigmoid, scale=-1.0)
 
-        def log(i, h):
-            nc.scalar.activation(out=logsig[i][:, h, :, :], in_=logsig[i][:, h, :, :], func=ACT.Ln, bias=ln_floor[:])
+        def log(i, h, sides=slice(0, 2)):
+            nc.scalar.activation(out=logsig[i][:, h, sides, :], in_=logsig[i][:, h, sides, :], func=ACT.Ln, bias=ln_floor[:])
 
-        def subtract(i):
-            gap[i] = work.tile([P, DIM], F32, name="gap", bufs=TILES)
-            nc.vector.tensor_tensor(
-                out=gap[i][:].rearrange("s (h t p) -> s h t p", h=PASSES, t=4),
-                in0=prev_rows[i].rearrange("s (h p t) -> s h t p", h=PASSES, t=4),
-                in1=delta_rows[i].rearrange("s (h p t) -> s h t p", h=PASSES, t=4),
-                op=ALU.subtract,
+        def by_pass_slot(rows):
+            return rows.rearrange("s (h p t) -> s h t p", h=PASSES, t=4)
+
+        def subtract(i, part, engine):
+            ts = PARTS[part]
+            gap[i, part] = work.tile([P, PASSES, ts.stop - ts.start, P], F32, name="gap%d" % part, bufs=(TILES, 1)[part])
+            engine.tensor_tensor(
+                out=gap[i, part][:], in0=by_pass_slot(prev_rows[i])[:, :, ts, :],
+                in1=by_pass_slot(delta_rows[i])[:, :, ts, :], op=ALU.subtract,
             )
 
-        def r_group(h, c):
-            r_grouped[h, c] = work.tile([P, KP, 4], BF16, name="r_grouped", align_bytes=64)
-            nc.vector.tensor_copy(
-                out=r_grouped[h, c][:].rearrange("p (c i) t -> p c t i", i=4),
-                in_=r_raw[h][:, :, c * KP:(c + 1) * KP].rearrange("p t (c i) -> p c t i", i=4),
+        def r_group(h, c, copy, cols=slice(0, KP)):
+            if cols.start == 0:
+                r_grouped[h, c] = work.tile([P, KP, 4], BF16, name="r_grouped", align_bytes=64)
+            copy(
+                out=r_grouped[h, c][:, cols, :].rearrange("p (c i) t -> p c t i", i=4),
+                in_=r_raw[h][:, :, c * KP + cols.start:c * KP + cols.stop].rearrange("p t (c i) -> p c t i", i=4),
             )
 
         def r_quantize(h, c):
@@ -178,25 +184,31 @@ def tile_notransactionbandhedgepnl_w4_kernel(tc, x_bytes, x_scale, wl_words, wl_
             )
 
         def lower_edge(i, h):
-            lower[i, h] = work.tile([P, KP], F32, name="lower")
+            if h == 0:
+                lower[i] = work.tile([P, PASSES, 4, P], F32, name="lower")
             nc.vector.scalar_tensor_tensor(
-                out=slots(lower[i, h][:]), in0=by_slot(ab[i, h, 0][:]), scalar=-1.0,
+                out=lower[i][:, h, :, :], in0=by_slot(ab[i, h, 0][:]), scalar=-1.0,
                 in1=slots(logsig[i][:, h, 0, :]), op0=ALU.mult, op1=ALU.min,
             )
 
         def upper_edge(i, h):
-            upper[i, h] = work.tile([P, KP], F32, name="upper")
+            if h == 0:
+                upper[i] = work.tile([P, PASSES, 4, P], F32, name="upper")
             nc.vector.scalar_tensor_tensor(
-                out=slots(upper[i, h][:]), in0=slots(logsig[i][:, h, 1, :]), scalar=-1.0,
+                out=upper[i][:, h, :, :], in0=slots(logsig[i][:, h, 1, :]), scalar=-1.0,
                 in1=by_slot(ab[i, h, 1][:]), op0=ALU.mult, op1=ALU.max,
             )
 
-        def clamp_below(i, h):
-            nc.vector.tensor_tensor(out=lower[i, h][:], in0=lower[i, h][:], in1=gap[i][:, h * KP:(h + 1) * KP], op=ALU.max)
+        def clamp_below(i, part):
+            nc.vector.tensor_tensor(out=gap[i, part][:], in0=gap[i, part][:], in1=lower[i][:, :, PARTS[part], :], op=ALU.max)
 
-        def clamp_above(i, h):
-            moved[i, h] = work.tile([P, KP], F32, name="moved", bufs=3)
-            nc.vector.tensor_tensor(out=moved[i, h][:], in0=lower[i, h][:], in1=upper[i, h][:], op=ALU.min)
+        def clamp_above(i, part, passes=slice(0, PASSES)):
+            if i not in moved:
+                moved[i] = work.tile([P, PASSES, 4, P], F32, name="moved")
+            nc.vector.tensor_tensor(
+                out=moved[i][:, passes, PARTS[part], :], in0=gap[i, part][:, passes, :, :],
+                in1=upper[i][:, passes, PARTS[part], :], op=ALU.min,
+            )
 
         def turn_delta(i, h):
             held[i, h] = psum.tile([P, 4, P], F32, name="held")
@@ -209,7 +221,7 @@ def tile_notransactionbandhedgepnl_w4_kernel(tc, x_bytes, x_scale, wl_words, wl_
         def turn_moved(i, h):
             for t in range(4):
                 nc.tensor.matmul(
-                    held[i, h][:, t, :], lhsT=moved[i, h][:, t * P:(t + 1) * P], rhs=ident32[:],
+                    held[i, h][:, t, :], lhsT=moved[i][:, h, t, :], rhs=ident32[:],
                     start=False, stop=(t == 3), is_transpose=True,
                 )
 
@@ -243,12 +255,11 @@ def tile_notransactionbandhedgepnl_w4_kernel(tc, x_bytes, x_scale, wl_words, wl_
                 in_=pos[i][:, passes, :, :].rearrange("p h s t -> p (h s t)"),
             )
 
-        def settle_pass(i, c, h):
-            cols = slice(c * KP, (c + 1) * KP)
+        def settle_pass(i, cols, h, tag, bufs):
             if h == 0:
-                sums[i, c] = psum.tile([P, KP], F32, name="acc", **(dict(tag="ab", bufs=4) if i == TILES - 1 else dict(tag="xo")))
+                sums[i, cols.start] = psum.tile([P, cols.stop - cols.start], F32, name="acc", tag=tag, bufs=bufs)
             nc.tensor.matmul_mx(
-                out=sums[i, c][:],
+                out=sums[i, cols.start][:],
                 lhsT=pos_codes[i][:, h * P:(h + 1) * P].bitcast(FP8X4),
                 lhsT_scale=pos_planes[i][:, h * P:(h + 1) * P],
                 rhs=r_codes[:, h, cols].bitcast(FP8X4),
@@ -257,21 +268,20 @@ def tile_notransactionbandhedgepnl_w4_kernel(tc, x_bytes, x_scale, wl_words, wl_
                 stop=(h == PASSES - 1),
             )
 
-        def settle(i):
-            for c in range(2):
-                for h in range(PASSES):
-                    settle_pass(i, c, h)
+        def settle_half(i, c):
+            for h in range(PASSES):
+                settle_pass(i, slice(c * KP, (c + 1) * KP), h, "xo", 2)
 
         def store(i):
             result = work.tile([P, DIM], F32, name="result")
             for c in range(2):
-                nc.scalar.copy(out=result[:, c * KP:(c + 1) * KP], in_=sums[i, c][:])
+                nc.scalar.copy(out=result[:, c * KP:(c + 1) * KP], in_=sums[i, c * KP][:])
             nc.sync.dma_start(out=out[i * P:(i + 1) * P, :], in_=result[:])
 
-        def store_half(i, c, copy):
-            half = work.tile([P, KP], F32, name="half")
-            copy(out=half[:], in_=sums[i, c][:])
-            nc.sync.dma_start(out=out[i * P:(i + 1) * P, c * KP:(c + 1) * KP], in_=half[:])
+        def store_piece(i, cols, copy):
+            piece = work.tile([P, cols.stop - cols.start], F32, name="piece", bufs=4)
+            copy(out=piece[:], in_=sums[i, cols.start][:])
+            nc.sync.dma_start(out=out[i * P:(i + 1) * P, cols], in_=piece[:])
 
         for h in range(PASSES):
             spread_scale(h)
@@ -285,38 +295,47 @@ def tile_notransactionbandhedgepnl_w4_kernel(tc, x_bytes, x_scale, wl_words, wl_
         x_multiply(2)
         x_quantize(1)
         x_multiply(3)
-        r_pieces = [(h, c) for c in range(2) for h in range(PASSES)]
         for i in range(TILES):
+            pair = i % 2 == 0 and i + 2 < TILES
             for w in range(2):
                 for h in range(PASSES):
                     project(i, h, w)
                     sigmoid(i, h, w)
-                if w == 0 and i + 2 < TILES:
-                    x_turn(i + 2)
-            if i + 2 < TILES:
-                x_group(i + 2, nc.scalar.copy)
-            if i + 4 < TILES:
-                x_multiply(i + 4)
-            if i >= 5:
-                r_quantize(*r_pieces[i - 5])
-            if i >= 4:
-                r_group(*r_pieces[i - 4])
-            if i + 2 < TILES:
+            if pair:
+                x_turn(i + 2)
+                x_turn(i + 3)
+                if i + 4 < TILES:
+                    x_multiply(i + 4)
+                else:
+                    r_group(0, 0, nc.vector.tensor_copy)
+                x_group(i + 2, nc.vector.tensor_copy)
+                x_group(i + 3, nc.vector.tensor_copy)
                 x_quantize(i + 2)
-            subtract(i)
-            if i in (1, 3):
-                prev_rows.extend(load_rows(prev, i + 3, 2, BF16, "prev_rows", 2))
+                subtract(i, 0, nc.vector)
+                x_quantize(i + 3)
+                subtract(i + 1, 0, nc.vector)
+                if i + 5 < TILES:
+                    x_multiply(i + 5)
+        r_group(1, 0, nc.vector.tensor_copy)
+        r_quantize(0, 0)
+        subtract(6, 0, nc.vector)
+        r_group(0, 1, nc.vector.tensor_copy)
+        r_quantize(1, 0)
+        subtract(7, 0, nc.vector)
+        r_group(1, 1, nc.vector.tensor_copy)
+        r_quantize(0, 1)
+        subtract(0, 1, nc.vector)
+        r_quantize(1, 1)
         nc.vector.tensor_copy(out=g_wide[:], in_=g_cols[:])
-        r_quantize(*r_pieces[3])
-        log(0, 0)
-        log(0, 1)
         for h in range(PASSES):
             for w in range(2):
+                log(0, h, slice(w, w + 1))
                 project(0, h, w)
 
         last = TILES - 1
         for i in range(TILES):
             if i >= 1:
+                subtract(i, 1, nc.gpsimd)
                 turn_moved(i - 1, 0)
                 turn_moved(i - 1, 1)
                 scale_by_g_scalar(i - 1, 1)
@@ -333,28 +352,33 @@ def tile_notransactionbandhedgepnl_w4_kernel(tc, x_bytes, x_scale, wl_words, wl_
             if i >= 1:
                 scale_by_g(i - 1, 0)
             if i >= 2:
-                settle(i - 2)
+                settle_half(i - 2, 0)
+                settle_half(i - 2, 1)
                 store(i - 2)
             turn_delta(i, 0)
             turn_delta(i, 1)
             clamp_below(i, 0)
             if i == last:
                 pos_quantize(i - 1, slice(0, 2))
-                settle(i - 1)
+                settle_half(i - 1, 0)
+                settle_half(i - 1, 1)
                 store(i - 1)
             clamp_below(i, 1)
-            clamp_above(i, 0)
-            if 1 <= i < last:
-                pos_quantize(i - 1, slice(0, 2))
-            if i == last:
-                turn_moved(i, 0)
-            clamp_above(i, 1)
-        turn_moved(last, 1)
+            if i < last:
+                clamp_above(i, 0)
+                if i >= 1:
+                    pos_quantize(i - 1, slice(0, 2))
+                clamp_above(i, 1)
+        for h in range(PASSES):
+            clamp_above(last, 0, slice(h, h + 1))
+            clamp_above(last, 1, slice(h, h + 1))
+            turn_moved(last, h)
         for h in range(PASSES):
             scale_by_g(last, h)
+        quarters = [slice(c * 256, (c + 1) * 256) for c in range(4)]
         for h in range(PASSES):
             pos_quantize(last, slice(h, h + 1))
-            for c in range(2):
-                settle_pass(last, c, h)
-        store_half(last, 0, nc.scalar.copy)
-        store_half(last, 1, nc.vector.tensor_copy)
+            for cols in quarters:
+                settle_pass(last, cols, h, "ab", 4)
+        for c, cols in enumerate(quarters):
+            store_piece(last, cols, (nc.scalar.copy, nc.vector.tensor_copy)[c % 2])

@@ -21,7 +21,6 @@ KP = 512
 PASSES = DIM // KP
 LN_FLOOR = 2.0 ** -60
 PARTS = (slice(0, 1), slice(1, 4))
-SCALAR_GROUPS = (0, 1)
 FLOPS = 3 * 2 * DIM * DIM * DIM
 
 
@@ -129,8 +128,8 @@ def tile_notransactionbandhedgepnl_w4_kernel(tc, x_bytes, x_scale, wl_words, wl_
             x_planes[i] = work.tile([P, PASSES * P], U8, name="x_planes", bufs=TILES, align_bytes=64)
             nc.vector.quantize_mx(out=x_codes[i][:].bitcast(FP8X4), scales=x_planes[i][:], in_=x_grouped[i][:])
 
-        def project(i, h, w):
-            ab[i, h, w] = psum.tile([P, KP], F32, name="ab", bufs=4)
+        def project(i, h, w, tag="ab", bufs=4):
+            ab[i, h, w] = psum.tile([P, KP], F32, name="ab", tag=tag, bufs=bufs)
             for k in range(PASSES):
                 nc.tensor.matmul_mx(
                     out=ab[i, h, w][:],
@@ -295,7 +294,8 @@ def tile_notransactionbandhedgepnl_w4_kernel(tc, x_bytes, x_scale, wl_words, wl_
         x_multiply(2)
         x_quantize(1)
         x_multiply(3)
-        for i in range(TILES):
+        last = TILES - 1
+        for i in range(last):
             pair = i % 2 == 0 and i + 2 < TILES
             for w in range(2):
                 for h in range(PASSES):
@@ -307,17 +307,19 @@ def tile_notransactionbandhedgepnl_w4_kernel(tc, x_bytes, x_scale, wl_words, wl_
                 if i + 4 < TILES:
                     x_multiply(i + 4)
                 else:
-                    r_group(0, 0, nc.vector.tensor_copy)
+                    r_group(1, 0, nc.vector.tensor_copy)
                 x_group(i + 2, nc.vector.tensor_copy)
-                x_group(i + 3, nc.vector.tensor_copy)
-                x_quantize(i + 2)
+                x_group(i + 3, nc.scalar.copy)
                 subtract(i, 0, nc.vector)
-                x_quantize(i + 3)
+                x_quantize(i + 2)
                 subtract(i + 1, 0, nc.vector)
                 if i + 5 < TILES:
                     x_multiply(i + 5)
-        r_group(1, 0, nc.vector.tensor_copy)
-        r_quantize(0, 0)
+                else:
+                    r_quantize(0, 0)
+                x_quantize(i + 3)
+                if i == 2:
+                    r_group(0, 0, nc.vector.tensor_copy)
         subtract(6, 0, nc.vector)
         r_group(0, 1, nc.vector.tensor_copy)
         r_quantize(1, 0)
@@ -331,17 +333,30 @@ def tile_notransactionbandhedgepnl_w4_kernel(tc, x_bytes, x_scale, wl_words, wl_
             for w in range(2):
                 log(0, h, slice(w, w + 1))
                 project(0, h, w)
+        for h in range(PASSES):
+            project(last, h, 0, "xo", 2)
 
-        last = TILES - 1
         for i in range(TILES):
             if i >= 1:
                 subtract(i, 1, nc.gpsimd)
                 turn_moved(i - 1, 0)
                 turn_moved(i - 1, 1)
+            if i == 1:
+                for h in range(PASSES):
+                    project(last, h, 1, "xo", 2)
+                    sigmoid(last, h, 1)
+            if i >= 2:
                 scale_by_g_scalar(i - 1, 1)
-            if i < last:
+            if i == 1:
+                log(2, 0, slice(0, 1))
+                log(2, 0, slice(1, 2))
+                log(2, 1)
+            elif i < last:
                 log(i + 1, 0)
                 log(i + 1, 1)
+            if i == 0:
+                for h in range(PASSES):
+                    sigmoid(last, h, 0)
             for h in range(PASSES):
                 lower_edge(i, h)
                 upper_edge(i, h)
@@ -351,6 +366,8 @@ def tile_notransactionbandhedgepnl_w4_kernel(tc, x_bytes, x_scale, wl_words, wl_
                         project(i + 1, h, w)
             if i >= 1:
                 scale_by_g(i - 1, 0)
+            if i == 1:
+                scale_by_g(0, 1)
             if i >= 2:
                 settle_half(i - 2, 0)
                 settle_half(i - 2, 1)

from contextlib import ExitStack

import concourse.mybir as mybir
from concourse.masks import make_identity

F32 = mybir.dt.float32
BF16 = mybir.dt.bfloat16
I32 = mybir.dt.int32
U32 = mybir.dt.uint32
U8 = mybir.dt.uint8
FP8 = mybir.dt.float8_e4m3fn
FP8X4 = mybir.dt.float8_e4m3fn_x4
FP4X4 = mybir.dt.float4_e2m1fn_x4
ACT = mybir.ActivationFunctionType
ALU = mybir.AluOpType

P = 128
DIM = 1024
TILES = DIM // P
KP = 512
PASSES = DIM // KP
LN_FLOOR = 2.0 ** -60
PARTS = (slice(0, 1), slice(1, 4))
FLOPS = 3 * 2 * DIM * DIM * DIM


def tile_notransactionbandhedgepnl_w4_kernel(tc, x_bytes, x_scale, wl_words, wl_scales, wu_words, wu_scales, delta, prev, g, r, out):
    nc = tc.nc
    with ExitStack() as ctx:
        keep = ctx.enter_context(tc.tile_pool(name="keep", bufs=1))
        work = ctx.enter_context(tc.tile_pool(name="work", bufs=2))
        psum = ctx.enter_context(tc.psum_pool(name="psum", bufs=2))
        ctx.enter_context(tc.manual_schedule())

        ident32 = keep.tile([P, P], F32)
        nc.vector.memset(ident32[:], 0.0)
        w_words, w_planes = [], []
        for w in range(2):
            w_words.append(keep.tile([P, PASSES, 2 * DIM], U8, name="w_words%d" % w, align_bytes=64))
            w_planes.append(keep.tile([P, PASSES, DIM], U8, name="w_plane%d" % w, align_bytes=64))
            nc.vector.memset(w_planes[w][:].bitcast(I32), 0)
        ident16 = keep.tile([P, P], BF16)
        nc.vector.memset(ident16[:], 0.0)
        ln_floor = keep.tile([P, 1], F32)
        nc.vector.memset(ln_floor[:], LN_FLOOR)
        make_identity(nc, ident32[:], nomemset=True)
        make_identity(nc, ident16[:], nomemset=True)

        def load_rows(src, first, count, dtype, tag, bufs):
            dst = work.tile([P, count, DIM], dtype, name=tag, tag=tag, bufs=bufs)
            nc.sync.dma_start(out=dst[:], in_=src[first * P:(first + count) * P, :].rearrange("(n p) k -> p n k", p=P))
            return [dst[:, n, :] for n in range(count)]

        def load_words(w, words):
            nc.sync.dma_start(out=w_words[w][:].bitcast(I32), in_=words.rearrange("g p n -> p g n").bitcast(I32))

        def load_plane(w, scales):
            for q in range(4):
                nc.sync.dma_start(
                    out=w_planes[w][32 * q:32 * q + 4, :, :].bitcast(I32),
                    in_=scales[:, 4 * q:4 * q + 4, :].rearrange("g r n -> r g n").bitcast(I32),
                )

        scale_cols = keep.tile([P, PASSES, 4], F32)
        nc.sync.dma_start(out=scale_cols[:], in_=x_scale.rearrange("o (h p t) -> p (o h) t", p=P, t=4))
        x_rows = load_rows(x_bytes, 0, 1, U8, "xb_a", 1)
        load_words(0, wl_words)
        load_plane(0, wl_scales)
        x_rows = x_rows + load_rows(x_bytes, 1, 3, U8, "xb_b", 1)
        load_words(1, wu_words)
        load_plane(1, wu_scales)
        x_rows = x_rows + load_rows(x_bytes, 4, 4, U8, "xb_c", 1)
        delta_rows, prev_rows = [], []
        for pair in range(2):
            delta_rows.extend(load_rows(delta, 2 * pair, 2, BF16, "delta_rows", 4))
            prev_rows.extend(load_rows(prev, 2 * pair, 2, BF16, "prev_rows", 4))
        r_raw = []
        for h in range(PASSES):
            raw = keep.tile([P, 4, DIM], BF16, name="r_raw%d" % h)
            nc.sync.dma_start(out=raw[:], in_=r[h * KP:(h + 1) * KP, :].rearrange("(p t) j -> p t j", t=4))
            r_raw.append(raw)
        g_cols = keep.tile([P, PASSES, 4], BF16)
        nc.sync.dma_start(out=g_cols[:], in_=g.rearrange("(h p t) -> p h t", p=P, t=4))
        for pair in range(2, 4):
            delta_rows.extend(load_rows(delta, 2 * pair, 2, BF16, "delta_rows", 4))
            prev_rows.extend(load_rows(prev, 2 * pair, 2, BF16, "prev_rows", 4))

        x_wide, x_turned, x_grouped, x_codes, x_planes = {}, {}, {}, {}, {}
        logsig, gap, lower, upper, moved, held, pos, pos_codes, pos_planes, ab, sums = {}, {}, {}, {}, {}, {}, {}, {}, {}, {}, {}
        r_grouped = {}
        g_wide = keep.tile([P, PASSES, 4], F32)
        r_codes = keep.tile([P, PASSES, DIM], U32, align_bytes=64)
        r_planes = keep.tile([P, PASSES, DIM], U8, align_bytes=64)

        scale_rows = keep.tile([P, PASSES, 2, P, 2], F32)

        def spread_scale(h):
            spread = psum.tile([P, 4, P], F32, name="spread", tag="ab", bufs=4)
            for t in range(4):
                nc.tensor.transpose(spread[:, t, :], scale_cols[:, h, t:t + 1].to_broadcast([P, P]), ident32[:])
            nc.scalar.copy(out=scale_rows[:, h, :, :, :], in_=spread[:].rearrange("s (u e) p -> s u p e", e=2))

        def x_multiply(i):
            x_wide[i] = work.tile([P, PASSES, 2, P, 2], BF16, name="x_wide", bufs=4)
            for h in range(PASSES):
                nc.vector.tensor_tensor(
                    out=x_wide[i][:, h, :, :, :],
                    in0=x_rows[i][:, h * KP:(h + 1) * KP].bitcast(FP8).rearrange("s (p u e) -> s u p e", u=2, e=2),
                    in1=scale_rows[:, h, :, :, :], op=ALU.mult,
                )

        def x_turn(i):
            x_turned[i] = psum.tile([P, PASSES, 2, P], F32, name="x_turned", tag="xo")
            words = x_wide[i][:].rearrange("s h u p e -> s h u (p e)").bitcast(F32)
            for h in range(PASSES):
                for u in range(2):
                    nc.tensor.transpose(x_turned[i][:, h, u, :], words[:, h, u, :], ident32[:])

        def x_group(i, copy):
            x_grouped[i] = work.tile([P, DIM], BF16, name="x_grouped", align_bytes=64)
            copy(
                out=x_grouped[i][:].bitcast(F32).rearrange("p (h s u) -> p h s u", h=PASSES, u=2),
                in_=x_turned[i][:].rearrange("p h u s -> p h s u"),
            )

        def x_quantize(i):
            x_codes[i] = work.tile([P, PASSES * P], U32, name="x_codes", bufs=TILES, align_bytes=64)
            x_planes[i] = work.tile([P, PASSES * P], U8, name="x_planes", bufs=TILES, align_bytes=64)
            nc.vector.quantize_mx(out=x_codes[i][:].bitcast(FP8X4), scales=x_planes[i][:], in_=x_grouped[i][:])

        def project(i, h, w, tag="ab", bufs=4):
            ab[i, h, w] = psum.tile([P, KP], F32, name="ab", tag=tag, bufs=bufs)
            for k in range(PASSES):
                nc.tensor.matmul_mx(
                    out=ab[i, h, w][:],
                    lhsT=x_codes[i][:, k * P:(k + 1) * P].bitcast(FP8X4),
                    lhsT_scale=x_planes[i][:, k * P:(k + 1) * P],
                    rhs=w_words[w][:, k, 2 * h * KP:2 * (h + 1) * KP].bitcast(FP4X4),
                    rhs_scale=w_planes[w][:, k, h * KP:(h + 1) * KP],
                    start=(k == 0),
                    stop=(k == PASSES - 1),
                )

        def by_slot(ap):
            return ap.rearrange("s (p t) -> s t p", t=4)

        def slots(ap):
            return ap.rearrange("s (t p) -> s t p", t=4)

        def sigmoid(i, h, w):
            if (h, w) == (0, 0):
                logsig[i] = work.tile([P, PASSES, 2, KP], F32, name="logsig", bufs=TILES)
            nc.scalar.activation(out=slots(logsig[i][:, h, w, :]), in_=by_slot(ab[i, h, w][:]), func=ACT.Sigmoid, scale=-1.0)

        def log(i, h, sides=slice(0, 2)):
            nc.scalar.activation(out=logsig[i][:, h, sides, :], in_=logsig[i][:, h, sides, :], func=ACT.Ln, bias=ln_floor[:])

        def by_pass_slot(rows):
            return rows.rearrange("s (h p t) -> s h t p", h=PASSES, t=4)

        def subtract(i, part, engine):
            ts = PARTS[part]
            gap[i, part] = work.tile([P, PASSES, ts.stop - ts.start, P], F32, name="gap%d" % part, bufs=(TILES, 1)[part])
            engine.tensor_tensor(
                out=gap[i, part][:], in0=by_pass_slot(prev_rows[i])[:, :, ts, :],
                in1=by_pass_slot(delta_rows[i])[:, :, ts, :], op=ALU.subtract,
            )

        def r_group(h, c, copy, cols=slice(0, KP)):
            if cols.start == 0:
                r_grouped[h, c] = work.tile([P, KP, 4], BF16, name="r_grouped", align_bytes=64)
            copy(
                out=r_grouped[h, c][:, cols, :].rearrange("p (c i) t -> p c t i", i=4),
                in_=r_raw[h][:, :, c * KP + cols.start:c * KP + cols.stop].rearrange("p t (c i) -> p c t i", i=4),
            )

        def r_quantize(h, c):
            cols = slice(c * KP, (c + 1) * KP)
            nc.vector.quantize_mx(
                out=r_codes[:, h, cols].bitcast(FP8X4),
                scales=r_planes[:, h, cols],
                in_=r_grouped[h, c][:].rearrange("p j t -> p (j t)"),
            )

        def lower_edge(i, h):
            if h == 0:
                lower[i] = work.tile([P, PASSES, 4, P], F32, name="lower")
            nc.vector.scalar_tensor_tensor(
                out=lower[i][:, h, :, :], in0=by_slot(ab[i, h, 0][:]), scalar=-1.0,
                in1=slots(logsig[i][:, h, 0, :]), op0=ALU.mult, op1=ALU.min,
            )

        def upper_edge(i, h):
            if h == 0:
                upper[i] = work.tile([P, PASSES, 4, P], F32, name="upper")
            nc.vector.scalar_tensor_tensor(
                out=upper[i][:, h, :, :], in0=slots(logsig[i][:, h, 1, :]), scalar=-1.0,
                in1=by_slot(ab[i, h, 1][:]), op0=ALU.mult, op1=ALU.max,
            )

        def clamp_below(i, part):
            nc.vector.tensor_tensor(out=gap[i, part][:], in0=gap[i, part][:], in1=lower[i][:, :, PARTS[part], :], op=ALU.max)

        def clamp_above(i, part, passes=slice(0, PASSES)):
            if i not in moved:
                moved[i] = work.tile([P, PASSES, 4, P], F32, name="moved")
            nc.vector.tensor_tensor(
                out=moved[i][:, passes, PARTS[part], :], in0=gap[i, part][:, passes, :, :],
                in1=upper[i][:, passes, PARTS[part], :], op=ALU.min,
            )

        def turn_delta(i, h):
            held[i, h] = psum.tile([P, 4, P], F32, name="held")
            for t in range(4):
                nc.tensor.matmul(
                    held[i, h][:, t, :], lhsT=delta_rows[i][:, h * KP + t:(h + 1) * KP:4], rhs=ident16[:],
                    start=(t == 0), stop=False,
                )

        def turn_moved(i, h):
            for t in range(4):
                nc.tensor.matmul(
                    held[i, h][:, t, :], lhsT=moved[i][:, h, t, :], rhs=ident32[:],
                    start=False, stop=(t == 3), is_transpose=True,
                )

        def pos_tile(i):
            if i not in pos:
                pos[i] = work.tile([P, PASSES, P, 4], BF16, name="pos", align_bytes=64)
            return pos[i]

        def scale_by_g(i, h):
            nc.vector.tensor_tensor(
                out=pos_tile(i)[:, h, :, :], in0=held[i, h][:].rearrange("p t s -> p s t"),
                in1=g_cols[:, h, :].unsqueeze(1).to_broadcast([P, P, 4]), op=ALU.mult,
            )

        def scale_by_g_scalar(i, h):
            apart = work.tile([P, 4, P], BF16, name="apart")
            for t in range(4):
                nc.scalar.activation(out=apart[:, t, :], in_=held[i, h][:, t, :], func=ACT.Copy, scale=g_wide[:, h, t:t + 1])
            nc.scalar.copy(
                out=pos_tile(i)[:, h, :, :].rearrange("p (c i) t -> p c t i", i=4),
                in_=apart[:].rearrange("p t (c i) -> p c t i", i=4),
            )

        def pos_quantize(i, passes):
            if i not in pos_codes:
                pos_codes[i] = work.tile([P, PASSES * P], U32, name="pos_codes", bufs=3, align_bytes=64)
                pos_planes[i] = work.tile([P, PASSES * P], U8, name="pos_planes", bufs=3, align_bytes=64)
            cols = slice(passes.start * P, passes.stop * P)
            nc.vector.quantize_mx(
                out=pos_codes[i][:, cols].bitcast(FP8X4), scales=pos_planes[i][:, cols],
                in_=pos[i][:, passes, :, :].rearrange("p h s t -> p (h s t)"),
            )

        def settle_pass(i, cols, h, tag, bufs):
            if h == 0:
                sums[i, cols.start] = psum.tile([P, cols.stop - cols.start], F32, name="acc", tag=tag, bufs=bufs)
            nc.tensor.matmul_mx(
                out=sums[i, cols.start][:],
                lhsT=pos_codes[i][:, h * P:(h + 1) * P].bitcast(FP8X4),
                lhsT_scale=pos_planes[i][:, h * P:(h + 1) * P],
                rhs=r_codes[:, h, cols].bitcast(FP8X4),
                rhs_scale=r_planes[:, h, cols],
                start=(h == 0),
                stop=(h == PASSES - 1),
            )

        def settle_half(i, c):
            for h in range(PASSES):
                settle_pass(i, slice(c * KP, (c + 1) * KP), h, "xo", 2)

        def store(i):
            result = work.tile([P, DIM], F32, name="result")
            for c in range(2):
                nc.scalar.copy(out=result[:, c * KP:(c + 1) * KP], in_=sums[i, c * KP][:])
            nc.sync.dma_start(out=out[i * P:(i + 1) * P, :], in_=result[:])

        def store_piece(i, cols, copy):
            piece = work.tile([P, cols.stop - cols.start], F32, name="piece", bufs=4)
            copy(out=piece[:], in_=sums[i, cols.start][:])
            nc.sync.dma_start(out=out[i * P:(i + 1) * P, cols], in_=piece[:])

        for h in range(PASSES):
            spread_scale(h)
        x_multiply(0)
        x_turn(0)
        x_group(0, nc.scalar.copy)
        x_multiply(1)
        x_turn(1)
        x_quantize(0)
        x_group(1, nc.vector.tensor_copy)
        x_multiply(2)
        x_quantize(1)
        x_multiply(3)
        last = TILES - 1
        for i in range(last):
            pair = i % 2 == 0 and i + 2 < TILES
            for w in range(2):
                for h in range(PASSES):
                    project(i, h, w)
                    sigmoid(i, h, w)
            if pair:
                x_turn(i + 2)
                x_turn(i + 3)
                if i + 4 < TILES:
                    x_multiply(i + 4)
                else:
                    r_group(1, 0, nc.vector.tensor_copy)
                x_group(i + 2, nc.vector.tensor_copy)
                x_group(i + 3, nc.scalar.copy)
                subtract(i, 0, nc.vector)
                x_quantize(i + 2)
                subtract(i + 1, 0, nc.vector)
                if i + 5 < TILES:
                    x_multiply(i + 5)
                else:
                    r_quantize(0, 0)
                x_quantize(i + 3)
                if i == 2:
                    r_group(0, 0, nc.vector.tensor_copy)
        subtract(6, 0, nc.vector)
        r_group(0, 1, nc.vector.tensor_copy)
        r_quantize(1, 0)
        subtract(7, 0, nc.vector)
        r_group(1, 1, nc.vector.tensor_copy)
        r_quantize(0, 1)
        subtract(0, 1, nc.vector)
        r_quantize(1, 1)
        nc.vector.tensor_copy(out=g_wide[:], in_=g_cols[:])
        for h in range(PASSES):
            for w in range(2):
                log(0, h, slice(w, w + 1))
                project(0, h, w)
        for h in range(PASSES):
            project(last, h, 0, "xo", 2)

        for i in range(TILES):
            if i >= 1:
                subtract(i, 1, nc.gpsimd)
                turn_moved(i - 1, 0)
                turn_moved(i - 1, 1)
            if i == 1:
                for h in range(PASSES):
                    project(last, h, 1, "xo", 2)
                    sigmoid(last, h, 1)
            if i >= 2:
                scale_by_g_scalar(i - 1, 1)
            if i == 1:
                log(2, 0, slice(0, 1))
                log(2, 0, slice(1, 2))
                log(2, 1)
            elif i < last:
                log(i + 1, 0)
                log(i + 1, 1)
            if i == 0:
                for h in range(PASSES):
                    sigmoid(last, h, 0)
            for h in range(PASSES):
                lower_edge(i, h)
                upper_edge(i, h)
            if i < last:
                for h in range(PASSES):
                    for w in range(2):
                        project(i + 1, h, w)
            if i >= 1:
                scale_by_g(i - 1, 0)
            if i == 1:
                scale_by_g(0, 1)
            if i >= 2:
                settle_half(i - 2, 0)
                settle_half(i - 2, 1)
                store(i - 2)
            turn_delta(i, 0)
            turn_delta(i, 1)
            clamp_below(i, 0)
            if i == last:
                pos_quantize(i - 1, slice(0, 2))
                settle_half(i - 1, 0)
                settle_half(i - 1, 1)
                store(i - 1)
            clamp_below(i, 1)
            if i < last:
                clamp_above(i, 0)
                if i >= 1:
                    pos_quantize(i - 1, slice(0, 2))
                clamp_above(i, 1)
        for h in range(PASSES):
            clamp_above(last, 0, slice(h, h + 1))
            clamp_above(last, 1, slice(h, h + 1))
            turn_moved(last, h)
        for h in range(PASSES):
            scale_by_g(last, h)
        quarters = [slice(c * 256, (c + 1) * 256) for c in range(4)]
        for h in range(PASSES):
            pos_quantize(last, slice(h, h + 1))
            for cols in quarters:
                settle_pass(last, cols, h, "ab", 4)
        for c, cols in enumerate(quarters):
            store_piece(last, cols, (nc.scalar.copy, nc.vector.tensor_copy)[c % 2])
